import numpy as np
import ml_dtypes


def mxq(x, axis, fmt="e4m3"):
    dtype, down = {"e4m3": (ml_dtypes.float8_e4m3fn, 7), "e5m2": (ml_dtypes.float8_e5m2, 14)}[fmt]
    v = np.moveaxis(np.asarray(x, np.float32).astype(ml_dtypes.bfloat16).astype(np.float64), axis, -1)
    blocks = v.reshape(v.shape[:-1] + (-1, 32))
    amax = np.abs(blocks).max(-1, keepdims=True)
    byte = np.maximum(np.where(amax > 0, np.frexp(amax)[1] - 1 + 127, 0) - down, 1)
    scale = np.exp2(byte - 127.0)
    codes = (blocks / scale).astype(np.float32).astype(dtype).astype(np.float64)
    return np.moveaxis((codes * scale).reshape(v.shape), -1, axis)


WIDE = False


def mx_kscale(k):
    if not WIDE:
        return np.ones(k)
    levels = np.array([30, -30])
    if k % 512:
        return np.exp2(np.random.permutation(np.resize(levels, k // 32))).repeat(32)
    a = np.empty((k // 512, 16))
    for p in range(k // 512):
        a[p, :8] = np.random.permutation(np.resize(levels, 8))
        for g in range(8):
            far = levels[np.abs(levels - a[p, g]) >= 10]
            a[p, g + 8] = far[np.random.randint(len(far))]
    return np.exp2(a.ravel()).repeat(32)


def f64(x):
    return np.asarray(x).astype(np.float64)


def striped(idx):
    return np.tile(np.asarray(idx).reshape(-1, 16).T, (8, 1)).astype(np.uint16)


def unstriped(offs):
    return offs[:16].T.reshape(-1).astype(np.int64)


E2M1 = np.array([0.0, 0.5, 1.0, 1.5, 2.0, 3.0, 4.0, 6.0, -0.0, -0.5, -1.0, -1.5, -2.0, -3.0, -4.0, -6.0])


def pack_weight(w, fmt):
    k, n = w.shape
    w = f64(np.asarray(w, np.float32).astype(ml_dtypes.bfloat16)).reshape(k // 32, 32, n)
    amax = np.abs(w).max(1)
    if fmt == "e4m3":
        byte = np.frexp(amax)[1] - 1 + 127 - 7
    else:
        mant, ex = np.frexp(amax / 6.0)
        byte = np.where(mant > 0.5, ex, ex - 1) + 127
    byte = np.clip(np.where(amax > 0, byte, 1), 1, 254)
    scaled = (w * np.exp2(127.0 - byte)[:, None, :]).reshape(k, n).astype(np.float32)
    by_word = np.ascontiguousarray(scaled.reshape(k // 512, 128, 4, n).transpose(0, 1, 3, 2))
    if fmt == "e4m3":
        words = by_word.astype(ml_dtypes.float8_e4m3fn).view(np.uint8)
    else:
        c = by_word.astype(ml_dtypes.float4_e2m1fn).view(np.uint8) & 0xF
        words = (c[..., 0::2] | (c[..., 1::2] << 4)).reshape(k // 512, 128, 2 * n)
    return np.ascontiguousarray(words), np.ascontiguousarray(byte.astype(np.uint8).reshape(k // 512, 16, n))


def unpack_weight(words, scales, fmt):
    g, _, n = scales.shape
    words = np.ascontiguousarray(words).reshape(g, 128, n, -1)
    if fmt == "e4m3":
        vals = words.view(ml_dtypes.float8_e4m3fn).astype(np.float64)
    else:
        nib = np.empty((g, 128, n, 4), np.uint8)
        nib[..., 0::2] = words & 0xF
        nib[..., 1::2] = words >> 4
        vals = E2M1[nib]
    vals = vals * np.repeat(np.exp2(scales.astype(np.float64) - 127.0), 8, axis=1)[..., None]
    return vals.transpose(0, 1, 3, 2).reshape(g * 512, n)


K, R, N, T, J = 512, 512, 512, 1024, 512


def setup_inputs():
    n = np.random.standard_normal
    idx = np.random.permutation(T)[:J]
    fn = mx_kscale(N)
    fr = mx_kscale(R)
    wdp = pack_weight(n((N, R)) * 1 / np.sqrt(N) * fn[:, None], "e4m3")
    wup = pack_weight(n((R, K)) * 1 / np.sqrt(R) / fr[:, None], "e2m1")
    return {
        "g": (n((N, T)) * np.exp(0.5 * n((1, T))) / fn[:, None]).astype(np.float32),
        "wd_words": wdp[0],
        "wd_scales": wdp[1],
        "us": (np.random.uniform(0.5, 2.0, (R, 1)) * fr[:, None]).astype(np.float32),
        "wu_words": wup[0],
        "wu_scales": wup[1],
        "offs": striped(idx),
    }


def reference(g, wd_words, wd_scales, us, wu_words, wu_scales, offs):
    idx = unstriped(offs)
    wdu = unpack_weight(wd_words, wd_scales, "e4m3")
    wuu = unpack_weight(wu_words, wu_scales, "e2m1")
    gidxq = mxq(f64(g)[:, idx], 0, "e5m2")
    dh = wdu.T @ gidxq
    dc = np.maximum(np.minimum(dh, 1.0), 0.0 - 1.0) * f64(us)
    dcq = mxq(dc, 0, "e5m2")
    y = wuu.T @ dcq
    return y

@@ -1,0 +1,192 @@
+from contextlib import ExitStack
+
+import concourse.mybir as mybir
+
+K, R, N, T, J = 512, 512, 512, 1024, 512
+FLOPS = 2 * N * R * J + 2 * R * K * J
+
+F32 = mybir.dt.float32
+BF16 = mybir.dt.bfloat16
+I32 = mybir.dt.int32
+U32 = mybir.dt.uint32
+U16 = mybir.dt.uint16
+U8 = mybir.dt.uint8
+E4M3X4 = mybir.dt.float8_e4m3fn_x4
+E5M2X4 = mybir.dt.float8_e5m2_x4
+E2M1X4 = mybir.dt.float4_e2m1fn_x4
+ALU = mybir.AluOpType
+ACT = mybir.ActivationFunctionType
+
+P = 128
+PACK = 4
+HALF = J // 2
+
+
+def load_scale_rows(queue, plane, rows):
+    for q in range(4):
+        queue.dma_start(out=plane[32 * q : 32 * q + 4, :].bitcast(I32), in_=rows[0, 4 * q : 4 * q + 4, :].bitcast(I32))
+
+
+def tile_list_clipped_back_kernel(tc, g, wd_words, wd_scales, us, wu_words, wu_scales, offs, out):
+    nc = tc.nc
+    with ExitStack() as ctx:
+        keep = ctx.enter_context(tc.tile_pool(name="keep", bufs=1))
+        reused = ctx.enter_context(tc.tile_pool(name="reused", bufs=1))
+        psum = ctx.enter_context(tc.psum_pool(name="psum", bufs=1))
+
+        def sb(name, shape, dtype):
+            return keep.tile(shape, dtype, name=name, align_bytes=64)
+
+        offsets = keep.tile([P, J // 16], U16, name="offsets")
+        g_rows = [sb(f"g_rows{t}", [P, T], F32) for t in range(PACK)]
+        wd_raw = sb("wd_raw", [P, R], U32)
+        wd_scale_raw = sb("wd_scale_raw", [P, R], U8)
+        wu_codes = sb("wu_codes", [P, 2 * K], U8)
+        wu_scale = sb("wu_scale", [P, K], U8)
+        factor = sb("factor", [P, PACK], F32)
+        upper = sb("upper", [P, PACK], F32)
+        lower = sb("lower", [P, PACK], F32)
+
+        nc.gpsimd.memset(wd_scale_raw[:].bitcast(U32), 0)
+        nc.gpsimd.memset(wu_scale[:].bitcast(U32), 0)
+
+        g_by_slot = g.rearrange("(p t) c -> p t c", t=PACK)
+        nc.sync.dma_start(out=g_rows[0][:], in_=g_by_slot[:, 0, :])
+        nc.sync.dma_start(offsets[:], offs)
+        for t in range(1, PACK):
+            nc.sync.dma_start(out=g_rows[t][:], in_=g_by_slot[:, t, :])
+        load_scale_rows(nc.sync, wd_scale_raw, wd_scales)
+        nc.sync.dma_start(out=wd_raw[:].bitcast(I32), in_=wd_words[0].rearrange("p n t -> p (n t)").bitcast(I32))
+        nc.sync.dma_start(out=factor[:], in_=us.rearrange("(p t) o -> p (t o)", t=PACK))
+        nc.sync.dma_start(out=wu_codes[:].bitcast(I32), in_=wu_words[0].bitcast(I32))
+        load_scale_rows(nc.sync, wu_scale, wu_scales)
+
+        picked_lo = sb("picked_lo", [P, 2, J], BF16)
+        picked_hi = [sb(f"picked_hi{h}", [P, 2, HALF], BF16) for h in range(2)]
+        g_woven = [
+            sb("g_woven0", [P, HALF, PACK], BF16),
+            reused.tile([P, HALF, PACK], BF16, name="g_woven1", align_bytes=64, offset=0),
+        ]
+        g_codes = sb("g_codes", [P, J], U32)
+        g_scale = sb("g_scale", [P, J], U8)
+
+        def half_list(h):
+            return offsets[:, h * (HALF // 16) : (h + 1) * (HALF // 16)]
+
+        def cols(h):
+            return slice(h * HALF, (h + 1) * HALF)
+
+        g_first = sb("g_first", [P, T], BF16)
+        nc.scalar.activation(out=g_first[:], in_=g_rows[0][:], func=ACT.Copy)
+        nc.scalar.activation(out=picked_lo[:, 0, :], in_=g_first[:].indirect(offsets[:]), func=ACT.Copy)
+        nc.vector.tensor_copy(out=picked_lo[:, 1, :], in_=g_rows[1][:].indirect(offsets[:]))
+        for h in range(2):
+            nc.scalar.copy(out=g_woven[h][:, :, 0:2], in_=picked_lo[:, :, cols(h)].rearrange("p t j -> p j t"))
+        for t in range(2, PACK):
+            for h in range(2):
+                nc.vector.tensor_copy(out=picked_hi[h][:, t - 2, :], in_=g_rows[t][:].indirect(half_list(h)))
+        nc.scalar.copy(out=g_woven[0][:, :, 2:4], in_=picked_hi[0][:].rearrange("p t j -> p j t"))
+        nc.vector.tensor_copy(out=g_woven[1][:, :, 2:4], in_=picked_hi[1][:].rearrange("p t j -> p j t"))
+
+        wd_codes = [sb("wd_codes0", [P, P], U32)] + [
+            reused.tile([P, P], U32, name=f"wd_codes{t}", align_bytes=64, offset=4 * P * (t - 1)) for t in range(1, PACK)
+        ]
+        wd_by_slot = wd_raw[:].rearrange("p (m t) -> p t m", t=PACK)
+        wd_scale = [sb("wd_scale0", [P, P], U8)] + [
+            reused.tile([P, P], U8, name=f"wd_scale{t}", align_bytes=64, offset=12 * P + P * (t - 1)) for t in range(1, PACK)
+        ]
+        wd_scale_by_slot = wd_scale_raw[:].rearrange("p (m t) -> p t m", t=PACK)
+
+        def deal_wd(t):
+            nc.vector.tensor_copy(out=wd_scale[t][:], in_=wd_scale_by_slot[:, t, :])
+            nc.vector.tensor_copy(out=wd_codes[t][:], in_=wd_by_slot[:, t, :])
+
+        nc.scalar.activation(out=upper[:], in_=factor[:], func=ACT.Abs)
+        nc.scalar.activation(out=lower[:], in_=upper[:], func=ACT.Copy, scale=-1.0)
+        deal_wd(0)
+        for h in range(2):
+            nc.vector.quantize_mx(
+                out=g_codes[:, cols(h)].bitcast(E5M2X4),
+                scales=g_scale[:, cols(h)],
+                in_=g_woven[h][:].rearrange("p j t -> p (j t)"),
+            )
+        for t in range(1, PACK):
+            deal_wd(t)
+
+        dh = [psum.tile([P, J], F32, name=f"dh{t}") for t in range(PACK)]
+        for t in range(PACK):
+            nc.tensor.matmul_mx(
+                out=dh[t][:],
+                lhsT=wd_codes[t][:].bitcast(E4M3X4),
+                lhsT_scale=wd_scale[t][:],
+                rhs=g_codes[:].bitcast(E5M2X4),
+                rhs_scale=g_scale[:],
+                start=True,
+                stop=True,
+            )
+
+        scaled = [sb(f"scaled{t}", [P, J], BF16) for t in range(PACK - 1)]
+        scaled_last = [sb(f"scaled_last{h}", [P, HALF], BF16) for h in range(2)]
+        held = [sb(f"held{h}", [P, 2, HALF, 2], BF16) for h in range(2)]
+        dc_woven = [sb(f"dc_woven{h}", [P, HALF, PACK], BF16) for h in range(2)]
+        dc_codes = sb("dc_codes", [P, J], U32)
+        dc_scale = sb("dc_scale", [P, J], U8)
+
+        def hold(dst, src, t):
+            nc.vector.tensor_scalar(
+                out=dst, in0=src, scalar1=upper[:, t : t + 1], scalar2=lower[:, t : t + 1], op0=ALU.min, op1=ALU.max
+            )
+
+        for t in range(PACK - 1):
+            nc.scalar.activation(out=scaled[t][:], in_=dh[t][:], func=ACT.Copy, scale=factor[:, t : t + 1])
+        for h in range(2):
+            nc.scalar.activation(out=scaled_last[h][:], in_=dh[3][:, cols(h)], func=ACT.Copy, scale=factor[:, 3:4])
+        for t in (3, 2):
+            nc.tensor.matmul_mx(
+                out=dh[t][:],
+                lhsT=wd_codes[t][:].bitcast(E4M3X4),
+                lhsT_scale=wd_scale[t][:],
+                rhs=g_codes[:].bitcast(E5M2X4),
+                rhs_scale=g_scale[:],
+                start=True,
+                stop=True,
+            )
+        for t in range(PACK - 1):
+            for h in range(2):
+                hold(held[h][:, t // 2, :, t % 2], scaled[t][:, cols(h)], t)
+        for h in range(2):
+            hold(held[h][:, 1, :, 1], scaled_last[h][:], 3)
+
+        def pair_words(h):
+            src = held[h][:].rearrange("p u j e -> p (u j e)").bitcast(F32).rearrange("p (u j) -> p j u", u=2)
+            dst = dc_woven[h][:].rearrange("p j t -> p (j t)").bitcast(F32).rearrange("p (j u) -> p j u", u=2)
+            return dst, src
+
+        nc.scalar.copy(*pair_words(0))
+        nc.vector.tensor_copy(*pair_words(1))
+        for h in range(2):
+            nc.vector.quantize_mx(
+                out=dc_codes[:, cols(h)].bitcast(E5M2X4),
+                scales=dc_scale[:, cols(h)],
+                in_=dc_woven[h][:].rearrange("p j t -> p (j t)"),
+            )
+
+        for c in range(K // P):
+            y = psum.tile([P, J], F32, name=f"y{c}")
+            nc.tensor.matmul_mx(
+                out=y[:],
+                lhsT=wu_codes[:, 2 * P * c : 2 * P * (c + 1)].bitcast(E2M1X4),
+                lhsT_scale=wu_scale[:, P * c : P * (c + 1)],
+                rhs=dc_codes[:].bitcast(E5M2X4),
+                rhs_scale=dc_scale[:],
+                start=True,
+                stop=True,
+            )
+            pieces = [cols(0), cols(1)] if c in (0, 3) else [slice(0, J)]
+            for i, piece in enumerate(pieces):
+                result = sb(f"result{c}_{i}", [P, piece.stop - piece.start], F32)
+                if c % 2 == 0:
+                    nc.scalar.copy(out=result[:], in_=y[:, piece])
+                else:
+                    nc.vector.tensor_copy(out=result[:], in_=y[:, piece])
+                nc.sync.dma_start(out=out[P * c : P * (c + 1), piece], in_=result[:])

@@ -47,31 +47,32 @@ def tile_list_clipped_back_kernel(tc, g, wd_words, wd_scales, us, wu_words, wu_s
         upper = sb("upper", [P, PACK], F32)
         lower = sb("lower", [P, PACK], F32)
 
-        nc.gpsimd.memset(wd_scale_raw[:].bitcast(U32), 0)
+        nc.vector.memset(wd_scale_raw[:].bitcast(U32), 0)
         nc.gpsimd.memset(wu_scale[:].bitcast(U32), 0)
 
         g_by_slot = g.rearrange("(p t) c -> p t c", t=PACK)
         nc.sync.dma_start(out=g_rows[0][:], in_=g_by_slot[:, 0, :])
         nc.sync.dma_start(offsets[:], offs)
+        load_scale_rows(nc.sync, wd_scale_raw, wd_scales)
         for t in range(1, PACK):
             nc.sync.dma_start(out=g_rows[t][:], in_=g_by_slot[:, t, :])
-        load_scale_rows(nc.sync, wd_scale_raw, wd_scales)
         nc.sync.dma_start(out=wd_raw[:].bitcast(I32), in_=wd_words[0].rearrange("p n t -> p (n t)").bitcast(I32))
         nc.sync.dma_start(out=factor[:], in_=us.rearrange("(p t) o -> p (t o)", t=PACK))
         nc.sync.dma_start(out=wu_codes[:].bitcast(I32), in_=wu_words[0].bitcast(I32))
         load_scale_rows(nc.sync, wu_scale, wu_scales)
 
+        wd_scale = sb("wd_scale", [P, PACK, P], U8)
+        nc.vector.tensor_copy(out=wd_scale[:].rearrange("p t m -> p m t"), in_=wd_scale_raw[:].rearrange("p (m t) -> p m t", t=PACK))
+
         picked_lo = sb("picked_lo", [P, 2, J], BF16)
-        picked_hi = [sb(f"picked_hi{h}", [P, 2, HALF], BF16) for h in range(2)]
+        runs = [slice(0, HALF), slice(HALF, HALF + P), slice(HALF + P, J)]
+        picked_hi = [sb(f"picked_hi{i}", [P, 2, run.stop - run.start], BF16) for i, run in enumerate(runs)]
         g_woven = [
             sb("g_woven0", [P, HALF, PACK], BF16),
             reused.tile([P, HALF, PACK], BF16, name="g_woven1", align_bytes=64, offset=0),
         ]
         g_codes = sb("g_codes", [P, J], U32)
         g_scale = sb("g_scale", [P, J], U8)
-
-        def half_list(h):
-            return offsets[:, h * (HALF // 16) : (h + 1) * (HALF // 16)]
 
         def cols(h):
             return slice(h * HALF, (h + 1) * HALF)
@@ -83,27 +84,18 @@ def tile_list_clipped_back_kernel(tc, g, wd_words, wd_scales, us, wu_words, wu_s
         for h in range(2):
             nc.scalar.copy(out=g_woven[h][:, :, 0:2], in_=picked_lo[:, :, cols(h)].rearrange("p t j -> p j t"))
         for t in range(2, PACK):
-            for h in range(2):
-                nc.vector.tensor_copy(out=picked_hi[h][:, t - 2, :], in_=g_rows[t][:].indirect(half_list(h)))
+            for i, run in enumerate(runs):
+                part = offsets[:, run.start // 16 : run.stop // 16]
+                nc.vector.tensor_copy(out=picked_hi[i][:, t - 2, :], in_=g_rows[t][:].indirect(part))
         nc.scalar.copy(out=g_woven[0][:, :, 2:4], in_=picked_hi[0][:].rearrange("p t j -> p j t"))
-        nc.vector.tensor_copy(out=g_woven[1][:, :, 2:4], in_=picked_hi[1][:].rearrange("p t j -> p j t"))
+        nc.scalar.copy(out=g_woven[1][:, 0:P, 2:4], in_=picked_hi[1][:].rearrange("p t j -> p j t"))
 
         wd_codes = [sb("wd_codes0", [P, P], U32)] + [
             reused.tile([P, P], U32, name=f"wd_codes{t}", align_bytes=64, offset=4 * P * (t - 1)) for t in range(1, PACK)
         ]
         wd_by_slot = wd_raw[:].rearrange("p (m t) -> p t m", t=PACK)
-        wd_scale = [sb("wd_scale0", [P, P], U8)] + [
-            reused.tile([P, P], U8, name=f"wd_scale{t}", align_bytes=64, offset=12 * P + P * (t - 1)) for t in range(1, PACK)
-        ]
-        wd_scale_by_slot = wd_scale_raw[:].rearrange("p (m t) -> p t m", t=PACK)
-
-        def deal_wd(t):
-            nc.vector.tensor_copy(out=wd_scale[t][:], in_=wd_scale_by_slot[:, t, :])
-            nc.vector.tensor_copy(out=wd_codes[t][:], in_=wd_by_slot[:, t, :])
-
-        nc.scalar.activation(out=upper[:], in_=factor[:], func=ACT.Abs)
-        nc.scalar.activation(out=lower[:], in_=upper[:], func=ACT.Copy, scale=-1.0)
-        deal_wd(0)
+        nc.vector.tensor_copy(out=wd_codes[0][:], in_=wd_by_slot[:, 0, :])
+        nc.vector.tensor_copy(out=g_woven[1][:, P:HALF, 2:4], in_=picked_hi[2][:].rearrange("p t j -> p j t"))
         for h in range(2):
             nc.vector.quantize_mx(
                 out=g_codes[:, cols(h)].bitcast(E5M2X4),
@@ -111,14 +103,17 @@ def tile_list_clipped_back_kernel(tc, g, wd_words, wd_scales, us, wu_words, wu_s
                 in_=g_woven[h][:].rearrange("p j t -> p (j t)"),
             )
         for t in range(1, PACK):
-            deal_wd(t)
+            nc.vector.tensor_copy(out=wd_codes[t][:], in_=wd_by_slot[:, t, :])
+
+        nc.scalar.activation(out=upper[:], in_=factor[:], func=ACT.Abs)
+        nc.scalar.activation(out=lower[:], in_=upper[:], func=ACT.Copy, scale=-1.0)
 
         dh = [psum.tile([P, J], F32, name=f"dh{t}") for t in range(PACK)]
         for t in range(PACK):
             nc.tensor.matmul_mx(
                 out=dh[t][:],
                 lhsT=wd_codes[t][:].bitcast(E4M3X4),
-                lhsT_scale=wd_scale[t][:],
+                lhsT_scale=wd_scale[:, t, :],
                 rhs=g_codes[:].bitcast(E5M2X4),
                 rhs_scale=g_scale[:],
                 start=True,
@@ -145,7 +140,7 @@ def tile_list_clipped_back_kernel(tc, g, wd_words, wd_scales, us, wu_words, wu_s
             nc.tensor.matmul_mx(
                 out=dh[t][:],
                 lhsT=wd_codes[t][:].bitcast(E4M3X4),
-                lhsT_scale=wd_scale[t][:],
+                lhsT_scale=wd_scale[:, t, :],
                 rhs=g_codes[:].bitcast(E5M2X4),
                 rhs_scale=g_scale[:],
                 start=True,

@@ -18,13 +18,32 @@ ALU = mybir.AluOpType
 ACT = mybir.ActivationFunctionType
 
 P = 128
-PACK = 4
+SLOTS = 4
+ENTRIES_PER_COLUMN = 16
 HALF = J // 2
+HALVES = [slice(0, HALF), slice(HALF, J)]
+RUNS = [slice(0, HALF), slice(HALF, HALF + HALF // 2), slice(HALF + HALF // 2, J)]
 
 
-def load_scale_rows(queue, plane, rows):
+def half_of(run):
+    h = run.start // HALF
+    return h, slice(run.start - h * HALF, run.stop - h * HALF)
+
+
+def load_scale_rows(nc, tile, rows):
     for q in range(4):
-        queue.dma_start(out=plane[32 * q : 32 * q + 4, :].bitcast(I32), in_=rows[0, 4 * q : 4 * q + 4, :].bitcast(I32))
+        nc.sync.dma_start(
+            out=tile[32 * q : 32 * q + 4, :].bitcast(I32), in_=rows[0, 4 * q : 4 * q + 4, :].bitcast(I32)
+        )
+
+
+def quantise_halves(nc, woven, codes, scale):
+    for h in range(2):
+        nc.vector.quantize_mx(
+            out=codes[:, HALVES[h]].bitcast(E5M2X4),
+            scales=scale[:, HALVES[h]],
+            in_=woven[h][:].rearrange("p j t -> p (j t)"),
+        )
 
 
 def tile_list_clipped_back_kernel(tc, g, wd_words, wd_scales, us, wu_words, wu_scales, offs, out):
@@ -37,79 +56,79 @@ def tile_list_clipped_back_kernel(tc, g, wd_words, wd_scales, us, wu_words, wu_s
         def sb(name, shape, dtype):
             return keep.tile(shape, dtype, name=name, align_bytes=64)
 
-        offsets = keep.tile([P, J // 16], U16, name="offsets")
-        g_rows = [sb(f"g_rows{t}", [P, T], F32) for t in range(PACK)]
+        offsets = keep.tile([P, J // ENTRIES_PER_COLUMN], U16, name="offsets")
+        g_rows = [sb(f"g_rows{t}", [P, T], F32) for t in range(SLOTS)]
         wd_raw = sb("wd_raw", [P, R], U32)
         wd_scale_raw = sb("wd_scale_raw", [P, R], U8)
         wu_codes = sb("wu_codes", [P, 2 * K], U8)
         wu_scale = sb("wu_scale", [P, K], U8)
-        factor = sb("factor", [P, PACK], F32)
-        upper = sb("upper", [P, PACK], F32)
-        lower = sb("lower", [P, PACK], F32)
+        factor = sb("factor", [P, SLOTS], F32)
 
         nc.vector.memset(wd_scale_raw[:].bitcast(U32), 0)
         nc.gpsimd.memset(wu_scale[:].bitcast(U32), 0)
 
-        g_by_slot = g.rearrange("(p t) c -> p t c", t=PACK)
+        g_by_slot = g.rearrange("(p t) c -> p t c", t=SLOTS)
         nc.sync.dma_start(out=g_rows[0][:], in_=g_by_slot[:, 0, :])
         nc.sync.dma_start(offsets[:], offs)
-        load_scale_rows(nc.sync, wd_scale_raw, wd_scales)
-        for t in range(1, PACK):
+        load_scale_rows(nc, wd_scale_raw, wd_scales)
+        for t in range(1, SLOTS):
             nc.sync.dma_start(out=g_rows[t][:], in_=g_by_slot[:, t, :])
-        nc.sync.dma_start(out=wd_raw[:].bitcast(I32), in_=wd_words[0].rearrange("p n t -> p (n t)").bitcast(I32))
-        nc.sync.dma_start(out=factor[:], in_=us.rearrange("(p t) o -> p (t o)", t=PACK))
+        nc.sync.dma_start(out=wd_raw[:].bitcast(I32), in_=wd_words[0].rearrange("p c t -> p (c t)").bitcast(I32))
+        nc.sync.dma_start(out=factor[:], in_=us.rearrange("(p t) o -> p (t o)", t=SLOTS))
         nc.sync.dma_start(out=wu_codes[:].bitcast(I32), in_=wu_words[0].bitcast(I32))
-        load_scale_rows(nc.sync, wu_scale, wu_scales)
+        load_scale_rows(nc, wu_scale, wu_scales)
 
-        wd_scale = sb("wd_scale", [P, PACK, P], U8)
-        nc.vector.tensor_copy(out=wd_scale[:].rearrange("p t m -> p m t"), in_=wd_scale_raw[:].rearrange("p (m t) -> p m t", t=PACK))
+        wd_scale = sb("wd_scale", [P, SLOTS, P], U8)
+        nc.vector.tensor_copy(
+            out=wd_scale[:].rearrange("p t m -> p m t"), in_=wd_scale_raw[:].rearrange("p (m t) -> p m t", t=SLOTS)
+        )
 
         picked_lo = sb("picked_lo", [P, 2, J], BF16)
-        runs = [slice(0, HALF), slice(HALF, HALF + P), slice(HALF + P, J)]
-        picked_hi = [sb(f"picked_hi{i}", [P, 2, run.stop - run.start], BF16) for i, run in enumerate(runs)]
+        picked_hi = sb("picked_hi", [P, 2, J], BF16)
         g_woven = [
-            sb("g_woven0", [P, HALF, PACK], BF16),
-            reused.tile([P, HALF, PACK], BF16, name="g_woven1", align_bytes=64, offset=0),
+            sb("g_woven0", [P, HALF, SLOTS], BF16),
+            reused.tile([P, HALF, SLOTS], BF16, name="g_woven1", align_bytes=64, offset=0),
         ]
         g_codes = sb("g_codes", [P, J], U32)
         g_scale = sb("g_scale", [P, J], U8)
 
-        def cols(h):
-            return slice(h * HALF, (h + 1) * HALF)
-
-        g_first = sb("g_first", [P, T], BF16)
-        nc.scalar.activation(out=g_first[:], in_=g_rows[0][:], func=ACT.Copy)
-        nc.scalar.activation(out=picked_lo[:, 0, :], in_=g_first[:].indirect(offsets[:]), func=ACT.Copy)
+        g_rows0_bf16 = sb("g_rows0_bf16", [P, T], BF16)
+        nc.scalar.activation(out=g_rows0_bf16[:], in_=g_rows[0][:], func=ACT.Copy)
+        nc.scalar.activation(out=picked_lo[:, 0, :], in_=g_rows0_bf16[:].indirect(offsets[:]), func=ACT.Copy)
         nc.vector.tensor_copy(out=picked_lo[:, 1, :], in_=g_rows[1][:].indirect(offsets[:]))
         for h in range(2):
-            nc.scalar.copy(out=g_woven[h][:, :, 0:2], in_=picked_lo[:, :, cols(h)].rearrange("p t j -> p j t"))
-        for t in range(2, PACK):
-            for i, run in enumerate(runs):
-                part = offsets[:, run.start // 16 : run.stop // 16]
-                nc.vector.tensor_copy(out=picked_hi[i][:, t - 2, :], in_=g_rows[t][:].indirect(part))
-        nc.scalar.copy(out=g_woven[0][:, :, 2:4], in_=picked_hi[0][:].rearrange("p t j -> p j t"))
-        nc.scalar.copy(out=g_woven[1][:, 0:P, 2:4], in_=picked_hi[1][:].rearrange("p t j -> p j t"))
+            nc.scalar.copy(out=g_woven[h][:, :, 0:2], in_=picked_lo[:, :, HALVES[h]].rearrange("p t j -> p j t"))
+        nc.vector.tensor_copy(out=picked_hi[:, 0, :], in_=g_rows[2][:].indirect(offsets[:]))
+        for run in RUNS:
+            entries = offsets[:, run.start // ENTRIES_PER_COLUMN : run.stop // ENTRIES_PER_COLUMN]
+            nc.vector.tensor_copy(out=picked_hi[:, 1, run], in_=g_rows[3][:].indirect(entries))
+
+        def weave_g_hi(copy, run):
+            h, inside = half_of(run)
+            copy(out=g_woven[h][:, inside, 2:4], in_=picked_hi[:, :, run].rearrange("p t j -> p j t"))
+
+        weave_g_hi(nc.scalar.copy, RUNS[0])
+        weave_g_hi(nc.scalar.copy, RUNS[1])
 
         wd_codes = [sb("wd_codes0", [P, P], U32)] + [
-            reused.tile([P, P], U32, name=f"wd_codes{t}", align_bytes=64, offset=4 * P * (t - 1)) for t in range(1, PACK)
+            reused.tile([P, P], U32, name=f"wd_codes{t}", align_bytes=64, offset=4 * P * (t - 1))
+            for t in range(1, SLOTS)
         ]
-        wd_by_slot = wd_raw[:].rearrange("p (m t) -> p t m", t=PACK)
+        wd_by_slot = wd_raw[:].rearrange("p (m t) -> p t m", t=SLOTS)
         nc.vector.tensor_copy(out=wd_codes[0][:], in_=wd_by_slot[:, 0, :])
-        nc.vector.tensor_copy(out=g_woven[1][:, P:HALF, 2:4], in_=picked_hi[2][:].rearrange("p t j -> p j t"))
-        for h in range(2):
-            nc.vector.quantize_mx(
-                out=g_codes[:, cols(h)].bitcast(E5M2X4),
-                scales=g_scale[:, cols(h)],
-                in_=g_woven[h][:].rearrange("p j t -> p (j t)"),
-            )
-        for t in range(1, PACK):
+        weave_g_hi(nc.vector.tensor_copy, RUNS[2])
+        quantise_halves(nc, g_woven, g_codes, g_scale)
+        for t in range(1, SLOTS):
             nc.vector.tensor_copy(out=wd_codes[t][:], in_=wd_by_slot[:, t, :])
 
+        upper = sb("upper", [P, SLOTS], F32)
+        lower = sb("lower", [P, SLOTS], F32)
         nc.scalar.activation(out=upper[:], in_=factor[:], func=ACT.Abs)
         nc.scalar.activation(out=lower[:], in_=upper[:], func=ACT.Copy, scale=-1.0)
 
-        dh = [psum.tile([P, J], F32, name=f"dh{t}") for t in range(PACK)]
-        for t in range(PACK):
+        dh = [psum.tile([P, J], F32, name=f"dh{t}") for t in range(SLOTS)]
+
+        def first_product(t):
             nc.tensor.matmul_mx(
                 out=dh[t][:],
                 lhsT=wd_codes[t][:].bitcast(E4M3X4),
@@ -120,53 +139,50 @@ def tile_list_clipped_back_kernel(tc, g, wd_words, wd_scales, us, wu_words, wu_s
                 stop=True,
             )
 
-        scaled = [sb(f"scaled{t}", [P, J], BF16) for t in range(PACK - 1)]
-        scaled_last = [sb(f"scaled_last{h}", [P, HALF], BF16) for h in range(2)]
-        held = [sb(f"held{h}", [P, 2, HALF, 2], BF16) for h in range(2)]
-        dc_woven = [sb(f"dc_woven{h}", [P, HALF, PACK], BF16) for h in range(2)]
+        for t in range(SLOTS):
+            first_product(t)
+
+        last = SLOTS - 1
+        scaled = [sb(f"scaled{t}", [P, J], F32) for t in range(SLOTS)]
+        for t in range(last):
+            nc.scalar.activation(out=scaled[t][:], in_=dh[t][:], func=ACT.Copy, scale=factor[:, t : t + 1])
+        for run in RUNS:
+            nc.scalar.activation(
+                out=scaled[last][:, run], in_=dh[last][:, run], func=ACT.Copy, scale=factor[:, last : last + 1]
+            )
+
+        for t in (last, last - 1):
+            first_product(t)
+
+        dc_pairs = sb("dc_pairs", [P, J * SLOTS], BF16)
+        dc_by_slot = dc_pairs[:].rearrange("p (h u j e) -> p u e h j", h=2, u=2, e=2)
+        dc_pair_words = dc_pairs[:].bitcast(F32).rearrange("p (h u j) -> p h j u", h=2, u=2)
+        dc_woven = [sb(f"dc_woven{h}", [P, HALF, SLOTS], BF16) for h in range(2)]
         dc_codes = sb("dc_codes", [P, J], U32)
         dc_scale = sb("dc_scale", [P, J], U8)
 
-        def hold(dst, src, t):
+        def clip(dst, src, t):
             nc.vector.tensor_scalar(
                 out=dst, in0=src, scalar1=upper[:, t : t + 1], scalar2=lower[:, t : t + 1], op0=ALU.min, op1=ALU.max
             )
 
-        for t in range(PACK - 1):
-            nc.scalar.activation(out=scaled[t][:], in_=dh[t][:], func=ACT.Copy, scale=factor[:, t : t + 1])
-        for h in range(2):
-            nc.scalar.activation(out=scaled_last[h][:], in_=dh[3][:, cols(h)], func=ACT.Copy, scale=factor[:, 3:4])
-        for t in (3, 2):
-            nc.tensor.matmul_mx(
-                out=dh[t][:],
-                lhsT=wd_codes[t][:].bitcast(E4M3X4),
-                lhsT_scale=wd_scale[:, t, :],
-                rhs=g_codes[:].bitcast(E5M2X4),
-                rhs_scale=g_scale[:],
-                start=True,
-                stop=True,
-            )
-        for t in range(PACK - 1):
-            for h in range(2):
-                hold(held[h][:, t // 2, :, t % 2], scaled[t][:, cols(h)], t)
-        for h in range(2):
-            hold(held[h][:, 1, :, 1], scaled_last[h][:], 3)
+        def weave_dc(copy, run):
+            h, inside = half_of(run)
+            words = dc_woven[h][:].rearrange("p j t -> p (j t)").bitcast(F32).rearrange("p (j u) -> p j u", u=2)
+            copy(out=words[:, inside, :], in_=dc_pair_words[:, h, inside, :])
 
-        def pair_words(h):
-            src = held[h][:].rearrange("p u j e -> p (u j e)").bitcast(F32).rearrange("p (u j) -> p j u", u=2)
-            dst = dc_woven[h][:].rearrange("p j t -> p (j t)").bitcast(F32).rearrange("p (j u) -> p j u", u=2)
-            return dst, src
+        for t in range(last):
+            clip(dc_by_slot[:, t // 2, t % 2, :, :], scaled[t][:].rearrange("p (h j) -> p h j", h=2), t)
+        for run in RUNS:
+            h, inside = half_of(run)
+            clip(dc_by_slot[:, last // 2, last % 2, h, inside], scaled[last][:, run], last)
+        weave_dc(nc.scalar.copy, RUNS[0])
+        weave_dc(nc.vector.tensor_copy, RUNS[1])
+        weave_dc(nc.vector.tensor_copy, RUNS[2])
+        quantise_halves(nc, dc_woven, dc_codes, dc_scale)
 
-        nc.scalar.copy(*pair_words(0))
-        nc.vector.tensor_copy(*pair_words(1))
-        for h in range(2):
-            nc.vector.quantize_mx(
-                out=dc_codes[:, cols(h)].bitcast(E5M2X4),
-                scales=dc_scale[:, cols(h)],
-                in_=dc_woven[h][:].rearrange("p j t -> p (j t)"),
-            )
-
-        for c in range(K // P):
+        banks = K // P
+        for c in range(banks):
             y = psum.tile([P, J], F32, name=f"y{c}")
             nc.tensor.matmul_mx(
                 out=y[:],
@@ -177,11 +193,9 @@ def tile_list_clipped_back_kernel(tc, g, wd_words, wd_scales, us, wu_words, wu_s
                 start=True,
                 stop=True,
             )
-            pieces = [cols(0), cols(1)] if c in (0, 3) else [slice(0, J)]
+            copy = nc.scalar.copy if c % 2 == 0 else nc.vector.tensor_copy
+            pieces = HALVES if c in (0, banks - 1) else [slice(0, J)]
             for i, piece in enumerate(pieces):
                 result = sb(f"result{c}_{i}", [P, piece.stop - piece.start], F32)
-                if c % 2 == 0:
-                    nc.scalar.copy(out=result[:], in_=y[:, piece])
-                else:
-                    nc.vector.tensor_copy(out=result[:], in_=y[:, piece])
+                copy(out=result[:], in_=y[:, piece])
                 nc.sync.dma_start(out=out[P * c : P * (c + 1), piece], in_=result[:])

from contextlib import ExitStack

import concourse.mybir as mybir

K, R, N, T, J = 512, 512, 512, 1024, 512
FLOPS = 2 * N * R * J + 2 * R * K * J

F32 = mybir.dt.float32
BF16 = mybir.dt.bfloat16
I32 = mybir.dt.int32
U32 = mybir.dt.uint32
U16 = mybir.dt.uint16
U8 = mybir.dt.uint8
E4M3X4 = mybir.dt.float8_e4m3fn_x4
E5M2X4 = mybir.dt.float8_e5m2_x4
E2M1X4 = mybir.dt.float4_e2m1fn_x4
ALU = mybir.AluOpType
ACT = mybir.ActivationFunctionType

P = 128
SLOTS = 4
ENTRIES_PER_COLUMN = 16
HALF = J // 2
HALVES = [slice(0, HALF), slice(HALF, J)]
RUNS = [slice(0, HALF), slice(HALF, HALF + HALF // 2), slice(HALF + HALF // 2, J)]


def half_of(run):
    h = run.start // HALF
    return h, slice(run.start - h * HALF, run.stop - h * HALF)


def load_scale_rows(nc, tile, rows):
    for q in range(4):
        nc.sync.dma_start(
            out=tile[32 * q : 32 * q + 4, :].bitcast(I32), in_=rows[0, 4 * q : 4 * q + 4, :].bitcast(I32)
        )


def quantise_halves(nc, woven, codes, scale):
    for h in range(2):
        nc.vector.quantize_mx(
            out=codes[:, HALVES[h]].bitcast(E5M2X4),
            scales=scale[:, HALVES[h]],
            in_=woven[h][:].rearrange("p j t -> p (j t)"),
        )


def tile_list_clipped_back_kernel(tc, g, wd_words, wd_scales, us, wu_words, wu_scales, offs, out):
    nc = tc.nc
    with ExitStack() as ctx:
        keep = ctx.enter_context(tc.tile_pool(name="keep", bufs=1))
        reused = ctx.enter_context(tc.tile_pool(name="reused", bufs=1))
        psum = ctx.enter_context(tc.psum_pool(name="psum", bufs=1))

        def sb(name, shape, dtype):
            return keep.tile(shape, dtype, name=name, align_bytes=64)

        offsets = keep.tile([P, J // ENTRIES_PER_COLUMN], U16, name="offsets")
        g_rows = [sb(f"g_rows{t}", [P, T], F32) for t in range(SLOTS)]
        wd_raw = sb("wd_raw", [P, R], U32)
        wd_scale_raw = sb("wd_scale_raw", [P, R], U8)
        wu_codes = sb("wu_codes", [P, 2 * K], U8)
        wu_scale = sb("wu_scale", [P, K], U8)
        factor = sb("factor", [P, SLOTS], F32)

        nc.vector.memset(wd_scale_raw[:].bitcast(U32), 0)
        nc.gpsimd.memset(wu_scale[:].bitcast(U32), 0)

        g_by_slot = g.rearrange("(p t) c -> p t c", t=SLOTS)
        nc.sync.dma_start(out=g_rows[0][:], in_=g_by_slot[:, 0, :])
        nc.sync.dma_start(offsets[:], offs)
        load_scale_rows(nc, wd_scale_raw, wd_scales)
        for t in range(1, SLOTS):
            nc.sync.dma_start(out=g_rows[t][:], in_=g_by_slot[:, t, :])
        nc.sync.dma_start(out=wd_raw[:].bitcast(I32), in_=wd_words[0].rearrange("p c t -> p (c t)").bitcast(I32))
        nc.sync.dma_start(out=factor[:], in_=us.rearrange("(p t) o -> p (t o)", t=SLOTS))
        nc.sync.dma_start(out=wu_codes[:].bitcast(I32), in_=wu_words[0].bitcast(I32))
        load_scale_rows(nc, wu_scale, wu_scales)

        wd_scale = sb("wd_scale", [P, SLOTS, P], U8)
        nc.vector.tensor_copy(
            out=wd_scale[:].rearrange("p t m -> p m t"), in_=wd_scale_raw[:].rearrange("p (m t) -> p m t", t=SLOTS)
        )

        picked_lo = sb("picked_lo", [P, 2, J], BF16)
        picked_hi = sb("picked_hi", [P, 2, J], BF16)
        g_woven = [
            sb("g_woven0", [P, HALF, SLOTS], BF16),
            reused.tile([P, HALF, SLOTS], BF16, name="g_woven1", align_bytes=64, offset=0),
        ]
        g_codes = sb("g_codes", [P, J], U32)
        g_scale = sb("g_scale", [P, J], U8)

        g_rows0_bf16 = sb("g_rows0_bf16", [P, T], BF16)
        nc.scalar.activation(out=g_rows0_bf16[:], in_=g_rows[0][:], func=ACT.Copy)
        nc.scalar.activation(out=picked_lo[:, 0, :], in_=g_rows0_bf16[:].indirect(offsets[:]), func=ACT.Copy)
        nc.vector.tensor_copy(out=picked_lo[:, 1, :], in_=g_rows[1][:].indirect(offsets[:]))
        for h in range(2):
            nc.scalar.copy(out=g_woven[h][:, :, 0:2], in_=picked_lo[:, :, HALVES[h]].rearrange("p t j -> p j t"))
        nc.vector.tensor_copy(out=picked_hi[:, 0, :], in_=g_rows[2][:].indirect(offsets[:]))
        for run in RUNS:
            entries = offsets[:, run.start // ENTRIES_PER_COLUMN : run.stop // ENTRIES_PER_COLUMN]
            nc.vector.tensor_copy(out=picked_hi[:, 1, run], in_=g_rows[3][:].indirect(entries))

        def weave_g_hi(copy, run):
            h, inside = half_of(run)
            copy(out=g_woven[h][:, inside, 2:4], in_=picked_hi[:, :, run].rearrange("p t j -> p j t"))

        weave_g_hi(nc.scalar.copy, RUNS[0])
        weave_g_hi(nc.scalar.copy, RUNS[1])

        wd_codes = [sb("wd_codes0", [P, P], U32)] + [
            reused.tile([P, P], U32, name=f"wd_codes{t}", align_bytes=64, offset=4 * P * (t - 1))
            for t in range(1, SLOTS)
        ]
        wd_by_slot = wd_raw[:].rearrange("p (m t) -> p t m", t=SLOTS)
        nc.vector.tensor_copy(out=wd_codes[0][:], in_=wd_by_slot[:, 0, :])
        weave_g_hi(nc.vector.tensor_copy, RUNS[2])
        quantise_halves(nc, g_woven, g_codes, g_scale)
        for t in range(1, SLOTS):
            nc.vector.tensor_copy(out=wd_codes[t][:], in_=wd_by_slot[:, t, :])

        upper = sb("upper", [P, SLOTS], F32)
        lower = sb("lower", [P, SLOTS], F32)
        nc.scalar.activation(out=upper[:], in_=factor[:], func=ACT.Abs)
        nc.scalar.activation(out=lower[:], in_=upper[:], func=ACT.Copy, scale=-1.0)

        dh = [psum.tile([P, J], F32, name=f"dh{t}") for t in range(SLOTS)]

        def first_product(t):
            nc.tensor.matmul_mx(
                out=dh[t][:],
                lhsT=wd_codes[t][:].bitcast(E4M3X4),
                lhsT_scale=wd_scale[:, t, :],
                rhs=g_codes[:].bitcast(E5M2X4),
                rhs_scale=g_scale[:],
                start=True,
                stop=True,
            )

        for t in range(SLOTS):
            first_product(t)

        last = SLOTS - 1
        scaled = [sb(f"scaled{t}", [P, J], F32) for t in range(SLOTS)]
        for t in range(last):
            nc.scalar.activation(out=scaled[t][:], in_=dh[t][:], func=ACT.Copy, scale=factor[:, t : t + 1])
        for run in RUNS:
            nc.scalar.activation(
                out=scaled[last][:, run], in_=dh[last][:, run], func=ACT.Copy, scale=factor[:, last : last + 1]
            )

        for t in (last, last - 1):
            first_product(t)

        dc_pairs = sb("dc_pairs", [P, J * SLOTS], BF16)
        dc_by_slot = dc_pairs[:].rearrange("p (h u j e) -> p u e h j", h=2, u=2, e=2)
        dc_pair_words = dc_pairs[:].bitcast(F32).rearrange("p (h u j) -> p h j u", h=2, u=2)
        dc_woven = [sb(f"dc_woven{h}", [P, HALF, SLOTS], BF16) for h in range(2)]
        dc_codes = sb("dc_codes", [P, J], U32)
        dc_scale = sb("dc_scale", [P, J], U8)

        def clip(dst, src, t):
            nc.vector.tensor_scalar(
                out=dst, in0=src, scalar1=upper[:, t : t + 1], scalar2=lower[:, t : t + 1], op0=ALU.min, op1=ALU.max
            )

        def weave_dc(copy, run):
            h, inside = half_of(run)
            words = dc_woven[h][:].rearrange("p j t -> p (j t)").bitcast(F32).rearrange("p (j u) -> p j u", u=2)
            copy(out=words[:, inside, :], in_=dc_pair_words[:, h, inside, :])

        for t in range(last):
            clip(dc_by_slot[:, t // 2, t % 2, :, :], scaled[t][:].rearrange("p (h j) -> p h j", h=2), t)
        for run in RUNS:
            h, inside = half_of(run)
            clip(dc_by_slot[:, last // 2, last % 2, h, inside], scaled[last][:, run], last)
        weave_dc(nc.scalar.copy, RUNS[0])
        weave_dc(nc.vector.tensor_copy, RUNS[1])
        weave_dc(nc.vector.tensor_copy, RUNS[2])
        quantise_halves(nc, dc_woven, dc_codes, dc_scale)

        banks = K // P
        for c in range(banks):
            y = psum.tile([P, J], F32, name=f"y{c}")
            nc.tensor.matmul_mx(
                out=y[:],
                lhsT=wu_codes[:, 2 * P * c : 2 * P * (c + 1)].bitcast(E2M1X4),
                lhsT_scale=wu_scale[:, P * c : P * (c + 1)],
                rhs=dc_codes[:].bitcast(E5M2X4),
                rhs_scale=dc_scale[:],
                start=True,
                stop=True,
            )
            copy = nc.scalar.copy if c % 2 == 0 else nc.vector.tensor_copy
            pieces = HALVES if c in (0, banks - 1) else [slice(0, J)]
            for i, piece in enumerate(pieces):
                result = sb(f"result{c}_{i}", [P, piece.stop - piece.start], F32)
                copy(out=result[:], in_=y[:, piece])
                nc.sync.dma_start(out=out[P * c : P * (c + 1), piece], in_=result[:])
